import numpy as np
import ml_dtypes


def mxq(x, axis, fmt="e4m3"):
    dtype, down = {"e4m3": (ml_dtypes.float8_e4m3fn, 7), "e5m2": (ml_dtypes.float8_e5m2, 14)}[fmt]
    v = np.moveaxis(np.asarray(x, np.float32).astype(ml_dtypes.bfloat16).astype(np.float64), axis, -1)
    blocks = v.reshape(v.shape[:-1] + (-1, 32))
    amax = np.abs(blocks).max(-1, keepdims=True)
    byte = np.maximum(np.where(amax > 0, np.frexp(amax)[1] - 1 + 127, 0) - down, 1)
    scale = np.exp2(byte - 127.0)
    codes = (blocks / scale).astype(np.float32).astype(dtype).astype(np.float64)
    return np.moveaxis((codes * scale).reshape(v.shape), -1, axis)


WIDE = False


def mx_kscale(k):
    if not WIDE:
        return np.ones(k)
    levels = np.array([10, -10, 5, -5, 0])
    if k % 512:
        return np.exp2(np.random.permutation(np.resize(levels, k // 32))).repeat(32)
    a = np.empty((k // 512, 16))
    for p in range(k // 512):
        a[p, :8] = np.random.permutation(np.resize(levels, 8))
        for g in range(8):
            far = levels[np.abs(levels - a[p, g]) >= 10]
            a[p, g + 8] = far[np.random.randint(len(far))]
    return np.exp2(a.ravel()).repeat(32)


def f64(x):
    return np.asarray(x).astype(np.float64)


def striped(idx):
    return np.tile(np.asarray(idx).reshape(-1, 16).T, (8, 1)).astype(np.uint16)


def unstriped(offs):
    return offs[:16].T.reshape(-1).astype(np.int64)


E2M1 = np.array([0.0, 0.5, 1.0, 1.5, 2.0, 3.0, 4.0, 6.0, -0.0, -0.5, -1.0, -1.5, -2.0, -3.0, -4.0, -6.0])


def pack_weight(w, fmt):
    k, n = w.shape
    w = f64(np.asarray(w, np.float32).astype(ml_dtypes.bfloat16)).reshape(k // 32, 32, n)
    amax = np.abs(w).max(1)
    if fmt == "e4m3":
        byte = np.frexp(amax)[1] - 1 + 127 - 7
    else:
        mant, ex = np.frexp(amax / 6.0)
        byte = np.where(mant > 0.5, ex, ex - 1) + 127
    byte = np.clip(np.where(amax > 0, byte, 1), 1, 254)
    scaled = (w * np.exp2(127.0 - byte)[:, None, :]).reshape(k, n).astype(np.float32)
    by_word = np.ascontiguousarray(scaled.reshape(k // 512, 128, 4, n).transpose(0, 1, 3, 2))
    if fmt == "e4m3":
        words = by_word.astype(ml_dtypes.float8_e4m3fn).view(np.uint8)
    else:
        c = by_word.astype(ml_dtypes.float4_e2m1fn).view(np.uint8) & 0xF
        words = (c[..., 0::2] | (c[..., 1::2] << 4)).reshape(k // 512, 128, 2 * n)
    return np.ascontiguousarray(words), np.ascontiguousarray(byte.astype(np.uint8).reshape(k // 512, 16, n))


def unpack_weight(words, scales, fmt):
    g, _, n = scales.shape
    words = np.ascontiguousarray(words).reshape(g, 128, n, -1)
    if fmt == "e4m3":
        vals = words.view(ml_dtypes.float8_e4m3fn).astype(np.float64)
    else:
        nib = np.empty((g, 128, n, 4), np.uint8)
        nib[..., 0::2] = words & 0xF
        nib[..., 1::2] = words >> 4
        vals = E2M1[nib]
    vals = vals * np.repeat(np.exp2(scales.astype(np.float64) - 127.0), 8, axis=1)[..., None]
    return vals.transpose(0, 1, 3, 2).reshape(g * 512, n)


def e4m3fn_bytes(y):
    return np.clip(np.asarray(y, np.float64), -448.0, 448.0).astype(np.float32).astype(ml_dtypes.float8_e4m3fn).view(np.uint8)


def e4m3fn_values(b):
    return np.asarray(b, np.uint8).view(ml_dtypes.float8_e4m3fn).astype(np.float64)


def sgn(shape):
    return np.random.uniform(0.5, 2.0, shape) * np.where(np.random.standard_normal(shape) < 0, -1.0, 1.0)


K, T, J, R, V, N, E = 512, 1024, 256, 512, 1024, 256, 512


def setup_inputs():
    n = np.random.standard_normal
    idx = np.random.permutation(T)[:J]
    idx2 = np.random.permutation(V)[:J]
    idx3 = np.random.permutation(V)[:J]
    idx4 = np.random.permutation(V)[:J]
    idx5 = np.random.permutation(E)[:J]
    fk = mx_kscale(K)
    fr = mx_kscale(R)
    xtp = pack_weight(n((K, T)) / fk[:, None], "e2m1")
    wp = pack_weight(n((K, R)) * 1 / np.sqrt(K) * fk[:, None], "e4m3")
    wbp = pack_weight(n((R, N)) * 1 / np.sqrt(R) / fr[:, None], "e2m1")
    return {
        "xt_words": xtp[0],
        "xt_scales": xtp[1],
        "w_words": wp[0],
        "w_scales": wp[1],
        "ca": e4m3fn_bytes(60.0 * n((R, V))),
        "st": (np.random.uniform(0.004, 0.012, (R, 1)) * fr[:, None]).astype(np.float32),
        "wb_words": wbp[0],
        "wb_scales": wbp[1],
        "so": (sgn((N, 1))).astype(np.float32),
        "offs": striped(idx),
        "offs2": striped(idx2),
        "offs3": striped(idx3),
        "offs4": striped(idx4),
        "offs5": striped(idx5),
    }


def reference(xt_words, xt_scales, w_words, w_scales, ca, st, wb_words, wb_scales, so, offs, offs2, offs3, offs4, offs5):
    idx = unstriped(offs)
    idx2 = unstriped(offs2)
    idx3 = unstriped(offs3)
    idx4 = unstriped(offs4)
    idx5 = unstriped(offs5)
    xtu = unpack_weight(xt_words, xt_scales, "e2m1")
    wu = unpack_weight(w_words, w_scales, "e4m3")
    wbu = unpack_weight(wb_words, wb_scales, "e2m1")
    xtidxg = xtu[:, idx]
    a = wu.T @ xtidxg
    m1 = np.maximum(np.minimum(e4m3fn_values(ca)[:, idx2], e4m3fn_values(ca)[:, idx3]), np.minimum(np.maximum(e4m3fn_values(ca)[:, idx2], e4m3fn_values(ca)[:, idx3]), e4m3fn_values(ca)[:, idx4]))
    g1 = m1 * f64(st)
    hid = a * g1
    hidq = mxq(hid, 0, "e4m3")
    p = wbu.T @ hidq
    y = np.zeros((N, E))
    y[:, idx5] = p * f64(so)
    return y

@@ -1,0 +1,163 @@
+from contextlib import ExitStack
+
+import concourse.mybir as mybir
+
+K, T, J, R, V, N, E = 512, 1024, 256, 512, 1024, 256, 512
+FLOPS = 2 * K * R * J + 2 * R * N * J
+
+F32 = mybir.dt.float32
+BF16 = mybir.dt.bfloat16
+I32 = mybir.dt.int32
+U32 = mybir.dt.uint32
+U16 = mybir.dt.uint16
+U8 = mybir.dt.uint8
+FP8 = mybir.dt.float8_e4m3fn
+FP8X4 = mybir.dt.float8_e4m3fn_x4
+FP4X4 = mybir.dt.float4_e2m1fn_x4
+ALU = mybir.AluOpType
+COPY = mybir.ActivationFunctionType.Copy
+
+P = 128
+PACK = 4
+HALF = J // 2
+RUN = 4
+
+
+def load_scale_rows(nc, plane, scales):
+    for q in range(4):
+        nc.sync.dma_start(
+            out=plane[32 * q : 32 * q + 4, :].bitcast(I32), in_=scales[0, 4 * q : 4 * q + 4, :].bitcast(I32)
+        )
+
+
+def tile_list_majority_kernel(
+    tc, xt_words, xt_scales, w_words, w_scales, ca, st, wb_words, wb_scales, so, offs, offs2, offs3, offs4, offs5, out
+):
+    nc = tc.nc
+    with ExitStack() as ctx:
+        keep = ctx.enter_context(tc.tile_pool(name="keep", bufs=1))
+        psum = ctx.enter_context(tc.psum_pool(name="psum", bufs=1))
+
+        def tile(name, shape, dtype, tag=""):
+            return keep.tile(shape, dtype, name=name, tag=tag or name, align_bytes=64)
+
+        xt_plane = tile("xt_plane", [P, T], U8)
+        w_plane = tile("w_plane", [P, R], U8)
+        wb_plane = tile("wb_plane", [P, N], U8)
+        for plane in (xt_plane, w_plane, wb_plane):
+            nc.vector.memset(plane[:].bitcast(I32), 0)
+        pages = [tile(f"page{c}", [P, E], F32) for c in range(2)]
+        for page in pages:
+            nc.gpsimd.memset(page[:], 0.0)
+
+        token_list = tile("token_list", [P, J // 16], U16)
+        vote_lists = [tile(f"vote_list{l}", [P, J // 16], U16) for l in range(3)]
+        page_list = tile("page_list", [P, J // 16], U16)
+        stores = [tile(f"store{t}", [P, V], U8) for t in range(PACK)]
+        ca_dealt = ca.rearrange("(p t) v -> p t v", t=PACK)
+        steps = tile("steps", [P, PACK], F32)
+        xt_table = tile("xt_table", [P, T], U16)
+        w_raw = tile("w_raw", [P, R], U32)
+        wb_codes = tile("wb_codes", [P, N], U16)
+        weights = tile("weights", [P, 2], F32)
+
+        nc.sync.dma_start(vote_lists[0][:], offs2)
+        nc.sync.dma_start(out=stores[0][:], in_=ca_dealt[:, 0, :])
+        nc.sync.dma_start(vote_lists[1][:], offs3)
+        nc.sync.dma_start(vote_lists[2][:], offs4)
+        nc.sync.dma_start(out=stores[1][:], in_=ca_dealt[:, 1, :])
+        nc.sync.dma_start(out=steps[:], in_=st.rearrange("(p t) o -> p (t o)", t=PACK))
+        nc.sync.dma_start(out=stores[2][:], in_=ca_dealt[:, 2, :])
+        nc.sync.dma_start(out=stores[3][:], in_=ca_dealt[:, 3, :])
+        nc.sync.dma_start(
+            out=w_raw[:].bitcast(I32), in_=w_words[0].rearrange("p c i -> p (c i)").bitcast(I32)
+        )
+        load_scale_rows(nc, w_plane, w_scales)
+        nc.sync.dma_start(token_list[:], offs)
+        nc.sync.dma_start(out=xt_table[:].bitcast(I32), in_=xt_words[0].bitcast(I32))
+        load_scale_rows(nc, xt_plane, xt_scales)
+        nc.sync.dma_start(out=wb_codes[:].bitcast(I32), in_=wb_words[0].bitcast(I32))
+        load_scale_rows(nc, wb_plane, wb_scales)
+        nc.sync.dma_start(page_list[:], offs5)
+        with nc.allow_non_contiguous_dma(reason="one float32 weight a partition and tile"):
+            nc.sync.dma_start(out=weights[:], in_=so.rearrange("(c p) o -> p (c o)", p=P))
+
+        votes = tile("votes", [P, PACK, 3 * J], F32)
+        for t in range(PACK):
+            picked = tile(f"picked{t}", [P, 3 * J], U8)
+            for l in range(3):
+                nc.vector.tensor_copy(picked[:, l * J : (l + 1) * J], stores[t][:].indirect(vote_lists[l][:]))
+            nc.scalar.activation(votes[:, t, :], picked[:].bitcast(FP8), COPY, scale=steps[:, t : t + 1])
+
+        w_codes = tile("w_codes", [P, R], U32)
+        w_dealt_plane = tile("w_dealt_plane", [P, R], U8)
+        nc.scalar.copy(
+            w_codes[:].rearrange("p (t m) -> p t m", t=PACK), w_raw[:].rearrange("p (m t) -> p t m", t=PACK)
+        )
+        nc.gpsimd.tensor_copy(
+            w_dealt_plane[:].rearrange("p (t m) -> p t m", t=PACK), w_plane[:].rearrange("p (m t) -> p t m", t=PACK)
+        )
+
+        x_codes = tile("x_codes", [P, J], U16)
+        x_plane = tile("x_plane", [P, J], U8)
+        nc.vector.tensor_copy(x_codes[:], xt_table[:].indirect(token_list[:]))
+        nc.vector.tensor_copy(x_plane[:], xt_plane[:].indirect(token_list[:]))
+
+        for h in range(2):
+            slots = slice(h * HALF, (h + 1) * HALF)
+            a = psum.tile([P, PACK, HALF], F32, name=f"a{h}")
+            for t in range(PACK):
+                cols = slice(t * P, (t + 1) * P)
+                nc.tensor.matmul_mx(
+                    out=a[:, t, :],
+                    lhsT=w_codes[:, cols].bitcast(FP8X4),
+                    lhsT_scale=w_dealt_plane[:, cols],
+                    rhs=x_codes[:, slots].bitcast(FP4X4),
+                    rhs_scale=x_plane[:, slots],
+                    start=True,
+                    stop=True,
+                )
+            first, second, third = [votes[:, :, l * J + h * HALF : l * J + (h + 1) * HALF] for l in range(3)]
+            high = tile(f"high{h}", [P, PACK, HALF], F32, tag="xt_table")
+            low = tile(f"low{h}", [P, PACK, HALF], F32, tag="xt_plane")
+            capped = tile(f"capped{h}", [P, PACK, HALF], F32)
+            gate = tile(f"gate{h}", [P, PACK, HALF], F32)
+            nc.vector.tensor_tensor(high[:], first, second, ALU.max)
+            nc.vector.tensor_tensor(low[:], first, second, ALU.min)
+            nc.vector.tensor_tensor(capped[:], high[:], third, ALU.min)
+            nc.vector.tensor_tensor(gate[:], low[:], capped[:], ALU.max)
+            hid = tile(f"hid{h}", [P, HALF * PACK], BF16)
+            nc.vector.tensor_tensor(
+                hid[:].rearrange("p (c i t) -> p c t i", i=RUN, t=PACK),
+                gate[:].rearrange("p t (c i) -> p c t i", i=RUN),
+                a[:].rearrange("p t (c i) -> p c t i", i=RUN),
+                ALU.mult,
+            )
+            hid_codes = tile(f"hid_codes{h}", [P, HALF], U32)
+            hid_plane = tile(f"hid_plane{h}", [P, HALF], U8)
+            nc.vector.quantize_mx(out=hid_codes[:].bitcast(FP8X4), scales=hid_plane[:], in_=hid[:])
+            for c in range(2):
+                cols = slice(c * P, (c + 1) * P)
+                sums = psum.tile([P, HALF], F32, name=f"sums{h}{c}")
+                nc.tensor.matmul_mx(
+                    out=sums[:],
+                    lhsT=wb_codes[:, cols].bitcast(FP4X4),
+                    lhsT_scale=wb_plane[:, cols],
+                    rhs=hid_codes[:].bitcast(FP8X4),
+                    rhs_scale=hid_plane[:],
+                    start=True,
+                    stop=True,
+                )
+                rows = tile(f"rows{h}{c}", [P, HALF], F32)
+                if h == 0:
+                    nc.scalar.copy(rows[:], sums[:])
+                else:
+                    nc.vector.tensor_copy(rows[:], sums[:])
+                nc.scalar.activation(
+                    pages[c][:].indirect(page_list[:, h * HALF // 16 : (h + 1) * HALF // 16]),
+                    rows[:],
+                    COPY,
+                    scale=weights[:, c : c + 1],
+                )
+        for c in range(2):
+            nc.sync.dma_start(out=out[c * P : (c + 1) * P, :], in_=pages[c][:])

@@ -21,6 +21,7 @@ P = 128
 PACK = 4
 HALF = J // 2
 RUN = 4
+QUARTER = J // 4
 
 
 def load_scale_rows(nc, plane, scales):
@@ -61,8 +62,8 @@ def tile_list_majority_kernel(
         wb_codes = tile("wb_codes", [P, N], U16)
         weights = tile("weights", [P, 2], F32)
 
-        nc.sync.dma_start(vote_lists[0][:], offs2)
         nc.sync.dma_start(out=stores[0][:], in_=ca_dealt[:, 0, :])
+        nc.sync.dma_start(vote_lists[0][:], offs2)
         nc.sync.dma_start(vote_lists[1][:], offs3)
         nc.sync.dma_start(vote_lists[2][:], offs4)
         nc.sync.dma_start(out=stores[1][:], in_=ca_dealt[:, 1, :])
@@ -82,12 +83,18 @@ def tile_list_majority_kernel(
         with nc.allow_non_contiguous_dma(reason="one float32 weight a partition and tile"):
             nc.sync.dma_start(out=weights[:], in_=so.rearrange("(c p) o -> p (c o)", p=P))
 
-        votes = tile("votes", [P, PACK, 3 * J], F32)
+        votes = tile("votes", [P, PACK, 3, J], F32)
+        apart = tile("apart", [P, PACK, 2, J], F32)
         for t in range(PACK):
             picked = tile(f"picked{t}", [P, 3 * J], U8)
             for l in range(3):
                 nc.vector.tensor_copy(picked[:, l * J : (l + 1) * J], stores[t][:].indirect(vote_lists[l][:]))
-            nc.scalar.activation(votes[:, t, :], picked[:].bitcast(FP8), COPY, scale=steps[:, t : t + 1])
+            nc.scalar.activation(
+                votes[:, t, :2, :].rearrange("p l j -> p (l j)"), picked[:, : 2 * J].bitcast(FP8), COPY
+            )
+            nc.scalar.activation(votes[:, t, 2, :], picked[:, 2 * J :].bitcast(FP8), COPY)
+            for l in range(2):
+                nc.gpsimd.tensor_tensor(apart[:, t, l, :], votes[:, t, l + 1, :], votes[:, t, 0, :], ALU.subtract)
 
         w_codes = tile("w_codes", [P, R], U32)
         w_dealt_plane = tile("w_dealt_plane", [P, R], U8)
@@ -98,66 +105,92 @@ def tile_list_majority_kernel(
             w_dealt_plane[:].rearrange("p (t m) -> p t m", t=PACK), w_plane[:].rearrange("p (m t) -> p t m", t=PACK)
         )
 
-        x_codes = tile("x_codes", [P, J], U16)
         x_plane = tile("x_plane", [P, J], U8)
-        nc.vector.tensor_copy(x_codes[:], xt_table[:].indirect(token_list[:]))
         nc.vector.tensor_copy(x_plane[:], xt_plane[:].indirect(token_list[:]))
+        x_codes = tile("x_codes", [P, J], U16, tag="xt_plane")
+        nc.vector.tensor_copy(x_codes[:], xt_table[:].indirect(token_list[:]))
 
-        for h in range(2):
-            slots = slice(h * HALF, (h + 1) * HALF)
-            a = psum.tile([P, PACK, HALF], F32, name=f"a{h}")
-            for t in range(PACK):
-                cols = slice(t * P, (t + 1) * P)
-                nc.tensor.matmul_mx(
-                    out=a[:, t, :],
-                    lhsT=w_codes[:, cols].bitcast(FP8X4),
-                    lhsT_scale=w_dealt_plane[:, cols],
-                    rhs=x_codes[:, slots].bitcast(FP4X4),
-                    rhs_scale=x_plane[:, slots],
-                    start=True,
-                    stop=True,
-                )
-            first, second, third = [votes[:, :, l * J + h * HALF : l * J + (h + 1) * HALF] for l in range(3)]
-            high = tile(f"high{h}", [P, PACK, HALF], F32, tag="xt_table")
-            low = tile(f"low{h}", [P, PACK, HALF], F32, tag="xt_plane")
-            capped = tile(f"capped{h}", [P, PACK, HALF], F32)
-            gate = tile(f"gate{h}", [P, PACK, HALF], F32)
-            nc.vector.tensor_tensor(high[:], first, second, ALU.max)
-            nc.vector.tensor_tensor(low[:], first, second, ALU.min)
-            nc.vector.tensor_tensor(capped[:], high[:], third, ALU.min)
-            nc.vector.tensor_tensor(gate[:], low[:], capped[:], ALU.max)
-            hid = tile(f"hid{h}", [P, HALF * PACK], BF16)
-            nc.vector.tensor_tensor(
-                hid[:].rearrange("p (c i t) -> p c t i", i=RUN, t=PACK),
-                gate[:].rearrange("p t (c i) -> p c t i", i=RUN),
-                a[:].rearrange("p t (c i) -> p c t i", i=RUN),
-                ALU.mult,
+        stepped = tile("stepped", [P, PACK, J], F32)
+        for t in range(PACK):
+            cols = slice(t * P, (t + 1) * P)
+            a = psum.tile([P, J], F32, name=f"a{t}")
+            nc.tensor.matmul_mx(
+                out=a[:],
+                lhsT=w_codes[:, cols].bitcast(FP8X4),
+                lhsT_scale=w_dealt_plane[:, cols],
+                rhs=x_codes[:].bitcast(FP4X4),
+                rhs_scale=x_plane[:],
+                start=True,
+                stop=True,
             )
-            hid_codes = tile(f"hid_codes{h}", [P, HALF], U32)
-            hid_plane = tile(f"hid_plane{h}", [P, HALF], U8)
-            nc.vector.quantize_mx(out=hid_codes[:].bitcast(FP8X4), scales=hid_plane[:], in_=hid[:])
+            nc.scalar.activation(stepped[:, t, :], a[:], COPY, scale=steps[:, t : t + 1])
+
+        hid = tile("hid", [P, J * PACK], BF16)
+        hid_codes = tile("hid_codes", [P, J], U32)
+        hid_plane = tile("hid_plane", [P, J], U8)
+
+        def gate_pair(quarters):
+            spans = [slice(k * QUARTER, (k + 1) * QUARTER) for k in quarters]
+            pair = tile(f"capped{quarters[0]}", [P, 2, PACK, QUARTER], F32, tag="xt_table")
+            capped = [pair[:, n] for n in range(2)]
+            clamped = [tile(f"clamped{k}", [P, PACK, QUARTER], F32) for k in quarters]
+            middle = [tile(f"middle{k}", [P, PACK, QUARTER], F32) for k in quarters]
+            for n, span in enumerate(spans):
+                nc.vector.scalar_tensor_tensor(
+                    capped[n], apart[:, :, 0, span], 0.0, apart[:, :, 1, span], ALU.max, ALU.min
+                )
+            for n, span in enumerate(spans):
+                nc.vector.scalar_tensor_tensor(clamped[n][:], apart[:, :, 0, span], 0.0, capped[n], ALU.min, ALU.max)
+            for n, span in enumerate(spans):
+                nc.vector.tensor_tensor(middle[n][:], clamped[n][:], votes[:, :, 0, span], ALU.add)
+            for n, span in enumerate(spans):
+                nc.vector.tensor_tensor(
+                    hid[:, PACK * span.start : PACK * span.stop].rearrange("p (c i t) -> p c t i", i=RUN, t=PACK),
+                    middle[n][:].rearrange("p t (c i) -> p c t i", i=RUN),
+                    stepped[:, :, span].rearrange("p t (c i) -> p c t i", i=RUN),
+                    ALU.mult,
+                )
+
+        def put(begin, end):
+            width = end - begin
+            nc.vector.quantize_mx(
+                out=hid_codes[:, begin:end].bitcast(FP8X4),
+                scales=hid_plane[:, begin:end],
+                in_=hid[:, PACK * begin : PACK * end],
+            )
+            if end == J:
+                sums = [psum.tile([P, HALF], F32, name=f"last{c}")[:] for c in range(2)]
+            else:
+                both = psum.tile([P, 2, HALF], F32, name=f"sums{begin}")
+                sums = [both[:, c, :] for c in range(2)]
+            rows = tile(f"rows{begin}", [P, 2, width], F32)
             for c in range(2):
                 cols = slice(c * P, (c + 1) * P)
-                sums = psum.tile([P, HALF], F32, name=f"sums{h}{c}")
                 nc.tensor.matmul_mx(
-                    out=sums[:],
+                    out=sums[c],
                     lhsT=wb_codes[:, cols].bitcast(FP4X4),
                     lhsT_scale=wb_plane[:, cols],
-                    rhs=hid_codes[:].bitcast(FP8X4),
-                    rhs_scale=hid_plane[:],
+                    rhs=hid_codes[:, end - HALF : end].bitcast(FP8X4),
+                    rhs_scale=hid_plane[:, end - HALF : end],
                     start=True,
                     stop=True,
                 )
-                rows = tile(f"rows{h}{c}", [P, HALF], F32)
-                if h == 0:
-                    nc.scalar.copy(rows[:], sums[:])
-                else:
-                    nc.vector.tensor_copy(rows[:], sums[:])
+                if end == J:
+                    nc.vector.tensor_copy(rows[:, c, :], sums[c][:, HALF - width :])
+            if end < J:
+                nc.scalar.copy(rows[:], both[:, :, HALF - width :])
+            for c in range(2):
                 nc.scalar.activation(
-                    pages[c][:].indirect(page_list[:, h * HALF // 16 : (h + 1) * HALF // 16]),
-                    rows[:],
+                    pages[c][:].indirect(page_list[:, begin // 16 : end // 16]),
+                    rows[:, c, :],
                     COPY,
                     scale=weights[:, c : c + 1],
                 )
-        for c in range(2):
-            nc.sync.dma_start(out=out[c * P : (c + 1) * P, :], in_=pages[c][:])
+
+        gate_pair((0, 1))
+        put(0, HALF)
+        gate_pair((2, 3))
+        put(HALF, 3 * QUARTER)
+        put(3 * QUARTER, J)
+        nc.sync.dma_start(out=out[:P, :], in_=pages[0][:])
+        nc.scalar.dma_start(out=out[P:, :], in_=pages[1][:])

@@ -45,11 +45,11 @@ def tile_list_majority_kernel(
         xt_plane = tile("xt_plane", [P, T], U8)
         w_plane = tile("w_plane", [P, R], U8)
         wb_plane = tile("wb_plane", [P, N], U8)
-        for plane in (xt_plane, w_plane, wb_plane):
-            nc.vector.memset(plane[:].bitcast(I32), 0)
+        for plane in (w_plane, xt_plane, wb_plane):
+            nc.gpsimd.memset(plane[:].bitcast(I32), 0)
         pages = [tile(f"page{c}", [P, E], F32) for c in range(2)]
         for page in pages:
-            nc.gpsimd.memset(page[:], 0.0)
+            nc.vector.memset(page[:], 0.0)
 
         token_list = tile("token_list", [P, J // 16], U16)
         vote_lists = [tile(f"vote_list{l}", [P, J // 16], U16) for l in range(3)]
@@ -66,35 +66,21 @@ def tile_list_majority_kernel(
         nc.sync.dma_start(vote_lists[0][:], offs2)
         nc.sync.dma_start(vote_lists[1][:], offs3)
         nc.sync.dma_start(vote_lists[2][:], offs4)
-        nc.sync.dma_start(out=stores[1][:], in_=ca_dealt[:, 1, :])
-        nc.sync.dma_start(out=steps[:], in_=st.rearrange("(p t) o -> p (t o)", t=PACK))
-        nc.sync.dma_start(out=stores[2][:], in_=ca_dealt[:, 2, :])
-        nc.sync.dma_start(out=stores[3][:], in_=ca_dealt[:, 3, :])
+        load_scale_rows(nc, w_plane, w_scales)
+        for t in range(1, PACK):
+            nc.sync.dma_start(out=stores[t][:], in_=ca_dealt[:, t, :])
         nc.sync.dma_start(
             out=w_raw[:].bitcast(I32), in_=w_words[0].rearrange("p c i -> p (c i)").bitcast(I32)
         )
-        load_scale_rows(nc, w_plane, w_scales)
         nc.sync.dma_start(token_list[:], offs)
         nc.sync.dma_start(out=xt_table[:].bitcast(I32), in_=xt_words[0].bitcast(I32))
         load_scale_rows(nc, xt_plane, xt_scales)
+        nc.sync.dma_start(out=steps[:], in_=st.rearrange("(p t) o -> p (t o)", t=PACK))
         nc.sync.dma_start(out=wb_codes[:].bitcast(I32), in_=wb_words[0].bitcast(I32))
         load_scale_rows(nc, wb_plane, wb_scales)
         nc.sync.dma_start(page_list[:], offs5)
         with nc.allow_non_contiguous_dma(reason="one float32 weight a partition and tile"):
             nc.sync.dma_start(out=weights[:], in_=so.rearrange("(c p) o -> p (c o)", p=P))
-
-        votes = tile("votes", [P, PACK, 3, J], F32)
-        apart = tile("apart", [P, PACK, 2, J], F32)
-        for t in range(PACK):
-            picked = tile(f"picked{t}", [P, 3 * J], U8)
-            for l in range(3):
-                nc.vector.tensor_copy(picked[:, l * J : (l + 1) * J], stores[t][:].indirect(vote_lists[l][:]))
-            nc.scalar.activation(
-                votes[:, t, :2, :].rearrange("p l j -> p (l j)"), picked[:, : 2 * J].bitcast(FP8), COPY
-            )
-            nc.scalar.activation(votes[:, t, 2, :], picked[:, 2 * J :].bitcast(FP8), COPY)
-            for l in range(2):
-                nc.gpsimd.tensor_tensor(apart[:, t, l, :], votes[:, t, l + 1, :], votes[:, t, 0, :], ALU.subtract)
 
         w_codes = tile("w_codes", [P, R], U32)
         w_dealt_plane = tile("w_dealt_plane", [P, R], U8)
@@ -105,27 +91,40 @@ def tile_list_majority_kernel(
             w_dealt_plane[:].rearrange("p (t m) -> p t m", t=PACK), w_plane[:].rearrange("p (m t) -> p t m", t=PACK)
         )
 
+        votes = tile("votes", [P, PACK, 3, J], F32)
+        apart = tile("apart", [P, PACK, 2, J], F32)
+        for t in range(PACK):
+            picked = tile(f"picked{t}", [P, 3 * J], U8)
+            for l in range(3):
+                nc.vector.tensor_copy(picked[:, l * J : (l + 1) * J], stores[t][:].indirect(vote_lists[l][:]))
+                nc.scalar.activation(votes[:, t, l, :], picked[:, l * J : (l + 1) * J].bitcast(FP8), COPY)
+            for l in range(2):
+                nc.gpsimd.tensor_tensor(apart[:, t, l, :], votes[:, t, l + 1, :], votes[:, t, 0, :], ALU.subtract)
+
         x_plane = tile("x_plane", [P, J], U8)
         nc.vector.tensor_copy(x_plane[:], xt_plane[:].indirect(token_list[:]))
         x_codes = tile("x_codes", [P, J], U16, tag="xt_plane")
         nc.vector.tensor_copy(x_codes[:], xt_table[:].indirect(token_list[:]))
 
-        stepped = tile("stepped", [P, PACK, J], F32)
-        for t in range(PACK):
-            cols = slice(t * P, (t + 1) * P)
-            a = psum.tile([P, J], F32, name=f"a{t}")
-            nc.tensor.matmul_mx(
-                out=a[:],
-                lhsT=w_codes[:, cols].bitcast(FP8X4),
-                lhsT_scale=w_dealt_plane[:, cols],
-                rhs=x_codes[:].bitcast(FP4X4),
-                rhs_scale=x_plane[:],
-                start=True,
-                stop=True,
-            )
-            nc.scalar.activation(stepped[:, t, :], a[:], COPY, scale=steps[:, t : t + 1])
+        stepped = [tile(f"stepped{h}", [P, PACK, HALF], F32) for h in range(2)]
+        banks = [psum.tile([P, 2, HALF], F32, name=f"a{t}") for t in range(PACK)]
+        for h in range(2):
+            slots = slice(h * HALF, (h + 1) * HALF)
+            for t in range(PACK):
+                cols = slice(t * P, (t + 1) * P)
+                nc.tensor.matmul_mx(
+                    out=banks[t][:, h, :],
+                    lhsT=w_codes[:, cols].bitcast(FP8X4),
+                    lhsT_scale=w_dealt_plane[:, cols],
+                    rhs=x_codes[:, slots].bitcast(FP4X4),
+                    rhs_scale=x_plane[:, slots],
+                    start=True,
+                    stop=True,
+                )
+                nc.scalar.activation(stepped[h][:, t, :], banks[t][:, h, :], COPY, scale=steps[:, t : t + 1])
 
-        hid = tile("hid", [P, J * PACK], BF16)
+        hid = [tile("hid0", [P, HALF * PACK], BF16)] + [tile(f"hid{k}", [P, QUARTER * PACK], BF16) for k in (2, 3)]
+        hid_parts = [hid[0][:, : QUARTER * PACK], hid[0][:, QUARTER * PACK :], hid[1][:], hid[2][:]]
         hid_codes = tile("hid_codes", [P, J], U32)
         hid_plane = tile("hid_plane", [P, J], U8)
 
@@ -145,52 +144,55 @@ def tile_list_majority_kernel(
                 nc.vector.tensor_tensor(middle[n][:], clamped[n][:], votes[:, :, 0, span], ALU.add)
             for n, span in enumerate(spans):
                 nc.vector.tensor_tensor(
-                    hid[:, PACK * span.start : PACK * span.stop].rearrange("p (c i t) -> p c t i", i=RUN, t=PACK),
+                    hid_parts[quarters[n]].rearrange("p (c i t) -> p c t i", i=RUN, t=PACK),
                     middle[n][:].rearrange("p t (c i) -> p c t i", i=RUN),
-                    stepped[:, :, span].rearrange("p t (c i) -> p c t i", i=RUN),
+                    stepped[quarters[n] // 2][:, :, n * QUARTER : (n + 1) * QUARTER].rearrange("p t (c i) -> p c t i", i=RUN),
                     ALU.mult,
                 )
 
-        def put(begin, end):
-            width = end - begin
+        def quantise(part, begin, end):
             nc.vector.quantize_mx(
-                out=hid_codes[:, begin:end].bitcast(FP8X4),
-                scales=hid_plane[:, begin:end],
-                in_=hid[:, PACK * begin : PACK * end],
+                out=hid_codes[:, begin:end].bitcast(FP8X4), scales=hid_plane[:, begin:end], in_=part[:]
             )
-            if end == J:
-                sums = [psum.tile([P, HALF], F32, name=f"last{c}")[:] for c in range(2)]
-            else:
-                both = psum.tile([P, 2, HALF], F32, name=f"sums{begin}")
-                sums = [both[:, c, :] for c in range(2)]
-            rows = tile(f"rows{begin}", [P, 2, width], F32)
-            for c in range(2):
-                cols = slice(c * P, (c + 1) * P)
-                nc.tensor.matmul_mx(
-                    out=sums[c],
-                    lhsT=wb_codes[:, cols].bitcast(FP4X4),
-                    lhsT_scale=wb_plane[:, cols],
-                    rhs=hid_codes[:, end - HALF : end].bitcast(FP8X4),
-                    rhs_scale=hid_plane[:, end - HALF : end],
-                    start=True,
-                    stop=True,
-                )
-                if end == J:
-                    nc.vector.tensor_copy(rows[:, c, :], sums[c][:, HALF - width :])
-            if end < J:
-                nc.scalar.copy(rows[:], both[:, :, HALF - width :])
-            for c in range(2):
-                nc.scalar.activation(
-                    pages[c][:].indirect(page_list[:, begin // 16 : end // 16]),
-                    rows[:, c, :],
-                    COPY,
-                    scale=weights[:, c : c + 1],
-                )
+
+        def product(sums, c, end):
+            cols = slice(c * P, (c + 1) * P)
+            nc.tensor.matmul_mx(
+                out=sums,
+                lhsT=wb_codes[:, cols].bitcast(FP4X4),
+                lhsT_scale=wb_plane[:, cols],
+                rhs=hid_codes[:, end - HALF : end].bitcast(FP8X4),
+                rhs_scale=hid_plane[:, end - HALF : end],
+                start=True,
+                stop=True,
+            )
+
+        def put(rows, c, begin, end):
+            nc.scalar.activation(
+                pages[c][:].indirect(page_list[:, begin // 16 : end // 16]), rows, COPY, scale=weights[:, c : c + 1]
+            )
 
         gate_pair((0, 1))
-        put(0, HALF)
+        quantise(hid[0], 0, HALF)
+        sums = psum.tile([P, 2, HALF], F32, name="sums_first")
+        rows = tile("rows_first", [P, 2, HALF], F32)
+        for c in range(2):
+            product(sums[:, c, :], c, HALF)
+        nc.scalar.copy(rows[:], sums[:])
+        for c in range(2):
+            put(rows[:, c, :], c, 0, HALF)
+
         gate_pair((2, 3))
-        put(HALF, 3 * QUARTER)
-        put(3 * QUARTER, J)
+        quantise(hid[1], HALF, 3 * QUARTER)
+        quantise(hid[2], 3 * QUARTER, J)
+        for c, begin, end in ((0, HALF, 3 * QUARTER), (0, 3 * QUARTER, J), (1, HALF, J)):
+            sums = psum.tile([P, HALF], F32, name=f"sums{c}{begin}")
+            rows = tile(f"rows{c}{begin}", [P, end - begin], F32)
+            product(sums[:], c, end)
+            if end < J:
+                nc.scalar.copy(rows[:], sums[:, HALF - (end - begin) :])
+            else:
+                nc.vector.tensor_copy(rows[:], sums[:, HALF - (end - begin) :])
+            put(rows[:], c, begin, end)
         nc.sync.dma_start(out=out[:P, :], in_=pages[0][:])
         nc.scalar.dma_start(out=out[P:, :], in_=pages[1][:])

@@ -16,12 +16,14 @@ FP8X4 = mybir.dt.float8_e4m3fn_x4
 FP4X4 = mybir.dt.float4_e2m1fn_x4
 ALU = mybir.AluOpType
 COPY = mybir.ActivationFunctionType.Copy
+LARGEST = 448.0
 
 P = 128
 PACK = 4
 HALF = J // 2
 RUN = 4
 QUARTER = J // 4
+EARLY = 2
 
 
 def load_scale_rows(nc, plane, scales):
@@ -67,14 +69,15 @@ def tile_list_majority_kernel(
         nc.sync.dma_start(vote_lists[1][:], offs3)
         nc.sync.dma_start(vote_lists[2][:], offs4)
         load_scale_rows(nc, w_plane, w_scales)
-        for t in range(1, PACK):
-            nc.sync.dma_start(out=stores[t][:], in_=ca_dealt[:, t, :])
+        nc.sync.dma_start(out=stores[1][:], in_=ca_dealt[:, 1, :])
+        nc.sync.dma_start(out=stores[2][:], in_=ca_dealt[:, 2, :])
         nc.sync.dma_start(
             out=w_raw[:].bitcast(I32), in_=w_words[0].rearrange("p c i -> p (c i)").bitcast(I32)
         )
         nc.sync.dma_start(token_list[:], offs)
-        nc.sync.dma_start(out=xt_table[:].bitcast(I32), in_=xt_words[0].bitcast(I32))
         load_scale_rows(nc, xt_plane, xt_scales)
+        nc.sync.dma_start(out=xt_table[:].bitcast(I32), in_=xt_words[0].bitcast(I32))
+        nc.sync.dma_start(out=stores[3][:], in_=ca_dealt[:, 3, :])
         nc.sync.dma_start(out=steps[:], in_=st.rearrange("(p t) o -> p (t o)", t=PACK))
         nc.sync.dma_start(out=wb_codes[:].bitcast(I32), in_=wb_words[0].bitcast(I32))
         load_scale_rows(nc, wb_plane, wb_scales)
@@ -91,20 +94,31 @@ def tile_list_majority_kernel(
             w_dealt_plane[:].rearrange("p (t m) -> p t m", t=PACK), w_plane[:].rearrange("p (m t) -> p t m", t=PACK)
         )
 
-        votes = tile("votes", [P, PACK, 3, J], F32)
-        apart = tile("apart", [P, PACK, 2, J], F32)
-        for t in range(PACK):
-            picked = tile(f"picked{t}", [P, 3 * J], U8)
+        votes = tile("votes", [P, 3, PACK, J], F32)
+        high = tile("high", [P, PACK, J], F32)
+        low = tile("low", [P, PACK, J], F32)
+
+        def look_up(t, tag=""):
+            picked = tile(f"picked{t}", [P, 3, J], U8, tag=tag)
             for l in range(3):
-                nc.vector.tensor_copy(picked[:, l * J : (l + 1) * J], stores[t][:].indirect(vote_lists[l][:]))
-                nc.scalar.activation(votes[:, t, l, :], picked[:, l * J : (l + 1) * J].bitcast(FP8), COPY)
-            for l in range(2):
-                nc.gpsimd.tensor_tensor(apart[:, t, l, :], votes[:, t, l + 1, :], votes[:, t, 0, :], ALU.subtract)
+                nc.vector.tensor_copy(picked[:, l, :], stores[t][:].indirect(vote_lists[l][:]))
+                nc.scalar.activation(votes[:, l, t, :], picked[:, l, :].bitcast(FP8), COPY)
+
+        for t in range(PACK - 1):
+            look_up(t)
+        for t in range(EARLY):
+            apart = tile(f"apart{t}", [P, J], F32)
+            excess = tile(f"excess{t}", [P, J], F32)
+            nc.gpsimd.tensor_tensor(apart[:], votes[:, 0, t, :], votes[:, 1, t, :], ALU.subtract)
+            nc.gpsimd.tensor_scalar(excess[:], apart[:], 2 * LARGEST, 0.0, ALU.min, ALU.max)
+            nc.gpsimd.tensor_tensor(high[:, t, :], votes[:, 1, t, :], excess[:], ALU.add)
+            nc.gpsimd.tensor_tensor(low[:, t, :], votes[:, 0, t, :], excess[:], ALU.subtract)
 
         x_plane = tile("x_plane", [P, J], U8)
         nc.vector.tensor_copy(x_plane[:], xt_plane[:].indirect(token_list[:]))
         x_codes = tile("x_codes", [P, J], U16, tag="xt_plane")
         nc.vector.tensor_copy(x_codes[:], xt_table[:].indirect(token_list[:]))
+        look_up(PACK - 1, tag="xt_table")
 
         stepped = [tile(f"stepped{h}", [P, PACK, HALF], F32) for h in range(2)]
         banks = [psum.tile([P, 2, HALF], F32, name=f"a{t}") for t in range(PACK)]
@@ -130,18 +144,17 @@ def tile_list_majority_kernel(
 
         def gate_pair(quarters):
             spans = [slice(k * QUARTER, (k + 1) * QUARTER) for k in quarters]
-            pair = tile(f"capped{quarters[0]}", [P, 2, PACK, QUARTER], F32, tag="xt_table")
+            half = slice(spans[0].start, spans[1].stop)
+            first, second = votes[:, 0, EARLY:, half], votes[:, 1, EARLY:, half]
+            nc.vector.tensor_tensor(high[:, EARLY:, half], first, second, ALU.max)
+            nc.vector.tensor_tensor(low[:, EARLY:, half], first, second, ALU.min)
+            pair = tile(f"capped{quarters[0]}", [P, 2, PACK, QUARTER], F32, tag="capped")
             capped = [pair[:, n] for n in range(2)]
-            clamped = [tile(f"clamped{k}", [P, PACK, QUARTER], F32) for k in quarters]
             middle = [tile(f"middle{k}", [P, PACK, QUARTER], F32) for k in quarters]
             for n, span in enumerate(spans):
-                nc.vector.scalar_tensor_tensor(
-                    capped[n], apart[:, :, 0, span], 0.0, apart[:, :, 1, span], ALU.max, ALU.min
-                )
+                nc.vector.tensor_tensor(capped[n], high[:, :, span], votes[:, 2, :, span], ALU.min)
             for n, span in enumerate(spans):
-                nc.vector.scalar_tensor_tensor(clamped[n][:], apart[:, :, 0, span], 0.0, capped[n], ALU.min, ALU.max)
-            for n, span in enumerate(spans):
-                nc.vector.tensor_tensor(middle[n][:], clamped[n][:], votes[:, :, 0, span], ALU.add)
+                nc.vector.tensor_tensor(middle[n][:], low[:, :, span], capped[n], ALU.max)
             for n, span in enumerate(spans):
                 nc.vector.tensor_tensor(
                     hid_parts[quarters[n]].rearrange("p (c i t) -> p c t i", i=RUN, t=PACK),

from contextlib import ExitStack

import concourse.mybir as mybir

K, T, J, R, V, N, E = 512, 1024, 256, 512, 1024, 256, 512
FLOPS = 2 * K * R * J + 2 * R * N * J

F32 = mybir.dt.float32
BF16 = mybir.dt.bfloat16
I32 = mybir.dt.int32
U32 = mybir.dt.uint32
U16 = mybir.dt.uint16
U8 = mybir.dt.uint8
FP8 = mybir.dt.float8_e4m3fn
FP8X4 = mybir.dt.float8_e4m3fn_x4
FP4X4 = mybir.dt.float4_e2m1fn_x4
ALU = mybir.AluOpType
COPY = mybir.ActivationFunctionType.Copy
LARGEST = 448.0

P = 128
PACK = 4
HALF = J // 2
RUN = 4
QUARTER = J // 4
EARLY = 2


def load_scale_rows(nc, plane, scales):
    for q in range(4):
        nc.sync.dma_start(
            out=plane[32 * q : 32 * q + 4, :].bitcast(I32), in_=scales[0, 4 * q : 4 * q + 4, :].bitcast(I32)
        )


def tile_list_majority_kernel(
    tc, xt_words, xt_scales, w_words, w_scales, ca, st, wb_words, wb_scales, so, offs, offs2, offs3, offs4, offs5, out
):
    nc = tc.nc
    with ExitStack() as ctx:
        keep = ctx.enter_context(tc.tile_pool(name="keep", bufs=1))
        psum = ctx.enter_context(tc.psum_pool(name="psum", bufs=1))

        def tile(name, shape, dtype, tag=""):
            return keep.tile(shape, dtype, name=name, tag=tag or name, align_bytes=64)

        xt_plane = tile("xt_plane", [P, T], U8)
        w_plane = tile("w_plane", [P, R], U8)
        wb_plane = tile("wb_plane", [P, N], U8)
        for plane in (w_plane, xt_plane, wb_plane):
            nc.gpsimd.memset(plane[:].bitcast(I32), 0)
        pages = [tile(f"page{c}", [P, E], F32) for c in range(2)]
        for page in pages:
            nc.vector.memset(page[:], 0.0)

        token_list = tile("token_list", [P, J // 16], U16)
        vote_lists = [tile(f"vote_list{l}", [P, J // 16], U16) for l in range(3)]
        page_list = tile("page_list", [P, J // 16], U16)
        stores = [tile(f"store{t}", [P, V], U8) for t in range(PACK)]
        ca_dealt = ca.rearrange("(p t) v -> p t v", t=PACK)
        steps = tile("steps", [P, PACK], F32)
        xt_table = tile("xt_table", [P, T], U16)
        w_raw = tile("w_raw", [P, R], U32)
        wb_codes = tile("wb_codes", [P, N], U16)
        weights = tile("weights", [P, 2], F32)

        nc.sync.dma_start(out=stores[0][:], in_=ca_dealt[:, 0, :])
        nc.sync.dma_start(vote_lists[0][:], offs2)
        nc.sync.dma_start(vote_lists[1][:], offs3)
        nc.sync.dma_start(vote_lists[2][:], offs4)
        load_scale_rows(nc, w_plane, w_scales)
        nc.sync.dma_start(out=stores[1][:], in_=ca_dealt[:, 1, :])
        nc.sync.dma_start(out=stores[2][:], in_=ca_dealt[:, 2, :])
        nc.sync.dma_start(
            out=w_raw[:].bitcast(I32), in_=w_words[0].rearrange("p c i -> p (c i)").bitcast(I32)
        )
        nc.sync.dma_start(token_list[:], offs)
        load_scale_rows(nc, xt_plane, xt_scales)
        nc.sync.dma_start(out=xt_table[:].bitcast(I32), in_=xt_words[0].bitcast(I32))
        nc.sync.dma_start(out=stores[3][:], in_=ca_dealt[:, 3, :])
        nc.sync.dma_start(out=steps[:], in_=st.rearrange("(p t) o -> p (t o)", t=PACK))
        nc.sync.dma_start(out=wb_codes[:].bitcast(I32), in_=wb_words[0].bitcast(I32))
        load_scale_rows(nc, wb_plane, wb_scales)
        nc.sync.dma_start(page_list[:], offs5)
        with nc.allow_non_contiguous_dma(reason="one float32 weight a partition and tile"):
            nc.sync.dma_start(out=weights[:], in_=so.rearrange("(c p) o -> p (c o)", p=P))

        w_codes = tile("w_codes", [P, R], U32)
        w_dealt_plane = tile("w_dealt_plane", [P, R], U8)
        nc.scalar.copy(
            w_codes[:].rearrange("p (t m) -> p t m", t=PACK), w_raw[:].rearrange("p (m t) -> p t m", t=PACK)
        )
        nc.gpsimd.tensor_copy(
            w_dealt_plane[:].rearrange("p (t m) -> p t m", t=PACK), w_plane[:].rearrange("p (m t) -> p t m", t=PACK)
        )

        votes = tile("votes", [P, 3, PACK, J], F32)
        high = tile("high", [P, PACK, J], F32)
        low = tile("low", [P, PACK, J], F32)

        def look_up(t, tag=""):
            picked = tile(f"picked{t}", [P, 3, J], U8, tag=tag)
            for l in range(3):
                nc.vector.tensor_copy(picked[:, l, :], stores[t][:].indirect(vote_lists[l][:]))
                nc.scalar.activation(votes[:, l, t, :], picked[:, l, :].bitcast(FP8), COPY)

        for t in range(PACK - 1):
            look_up(t)
        for t in range(EARLY):
            apart = tile(f"apart{t}", [P, J], F32)
            excess = tile(f"excess{t}", [P, J], F32)
            nc.gpsimd.tensor_tensor(apart[:], votes[:, 0, t, :], votes[:, 1, t, :], ALU.subtract)
            nc.gpsimd.tensor_scalar(excess[:], apart[:], 2 * LARGEST, 0.0, ALU.min, ALU.max)
            nc.gpsimd.tensor_tensor(high[:, t, :], votes[:, 1, t, :], excess[:], ALU.add)
            nc.gpsimd.tensor_tensor(low[:, t, :], votes[:, 0, t, :], excess[:], ALU.subtract)

        x_plane = tile("x_plane", [P, J], U8)
        nc.vector.tensor_copy(x_plane[:], xt_plane[:].indirect(token_list[:]))
        x_codes = tile("x_codes", [P, J], U16, tag="xt_plane")
        nc.vector.tensor_copy(x_codes[:], xt_table[:].indirect(token_list[:]))
        look_up(PACK - 1, tag="xt_table")

        stepped = [tile(f"stepped{h}", [P, PACK, HALF], F32) for h in range(2)]
        banks = [psum.tile([P, 2, HALF], F32, name=f"a{t}") for t in range(PACK)]
        for h in range(2):
            slots = slice(h * HALF, (h + 1) * HALF)
            for t in range(PACK):
                cols = slice(t * P, (t + 1) * P)
                nc.tensor.matmul_mx(
                    out=banks[t][:, h, :],
                    lhsT=w_codes[:, cols].bitcast(FP8X4),
                    lhsT_scale=w_dealt_plane[:, cols],
                    rhs=x_codes[:, slots].bitcast(FP4X4),
                    rhs_scale=x_plane[:, slots],
                    start=True,
                    stop=True,
                )
                nc.scalar.activation(stepped[h][:, t, :], banks[t][:, h, :], COPY, scale=steps[:, t : t + 1])

        hid = [tile("hid0", [P, HALF * PACK], BF16)] + [tile(f"hid{k}", [P, QUARTER * PACK], BF16) for k in (2, 3)]
        hid_parts = [hid[0][:, : QUARTER * PACK], hid[0][:, QUARTER * PACK :], hid[1][:], hid[2][:]]
        hid_codes = tile("hid_codes", [P, J], U32)
        hid_plane = tile("hid_plane", [P, J], U8)

        def gate_pair(quarters):
            spans = [slice(k * QUARTER, (k + 1) * QUARTER) for k in quarters]
            half = slice(spans[0].start, spans[1].stop)
            first, second = votes[:, 0, EARLY:, half], votes[:, 1, EARLY:, half]
            nc.vector.tensor_tensor(high[:, EARLY:, half], first, second, ALU.max)
            nc.vector.tensor_tensor(low[:, EARLY:, half], first, second, ALU.min)
            pair = tile(f"capped{quarters[0]}", [P, 2, PACK, QUARTER], F32, tag="capped")
            capped = [pair[:, n] for n in range(2)]
            middle = [tile(f"middle{k}", [P, PACK, QUARTER], F32) for k in quarters]
            for n, span in enumerate(spans):
                nc.vector.tensor_tensor(capped[n], high[:, :, span], votes[:, 2, :, span], ALU.min)
            for n, span in enumerate(spans):
                nc.vector.tensor_tensor(middle[n][:], low[:, :, span], capped[n], ALU.max)
            for n, span in enumerate(spans):
                nc.vector.tensor_tensor(
                    hid_parts[quarters[n]].rearrange("p (c i t) -> p c t i", i=RUN, t=PACK),
                    middle[n][:].rearrange("p t (c i) -> p c t i", i=RUN),
                    stepped[quarters[n] // 2][:, :, n * QUARTER : (n + 1) * QUARTER].rearrange("p t (c i) -> p c t i", i=RUN),
                    ALU.mult,
                )

        def quantise(part, begin, end):
            nc.vector.quantize_mx(
                out=hid_codes[:, begin:end].bitcast(FP8X4), scales=hid_plane[:, begin:end], in_=part[:]
            )

        def product(sums, c, end):
            cols = slice(c * P, (c + 1) * P)
            nc.tensor.matmul_mx(
                out=sums,
                lhsT=wb_codes[:, cols].bitcast(FP4X4),
                lhsT_scale=wb_plane[:, cols],
                rhs=hid_codes[:, end - HALF : end].bitcast(FP8X4),
                rhs_scale=hid_plane[:, end - HALF : end],
                start=True,
                stop=True,
            )

        def put(rows, c, begin, end):
            nc.scalar.activation(
                pages[c][:].indirect(page_list[:, begin // 16 : end // 16]), rows, COPY, scale=weights[:, c : c + 1]
            )

        gate_pair((0, 1))
        quantise(hid[0], 0, HALF)
        sums = psum.tile([P, 2, HALF], F32, name="sums_first")
        rows = tile("rows_first", [P, 2, HALF], F32)
        for c in range(2):
            product(sums[:, c, :], c, HALF)
        nc.scalar.copy(rows[:], sums[:])
        for c in range(2):
            put(rows[:, c, :], c, 0, HALF)

        gate_pair((2, 3))
        quantise(hid[1], HALF, 3 * QUARTER)
        quantise(hid[2], 3 * QUARTER, J)
        for c, begin, end in ((0, HALF, 3 * QUARTER), (0, 3 * QUARTER, J), (1, HALF, J)):
            sums = psum.tile([P, HALF], F32, name=f"sums{c}{begin}")
            rows = tile(f"rows{c}{begin}", [P, end - begin], F32)
            product(sums[:], c, end)
            if end < J:
                nc.scalar.copy(rows[:], sums[:, HALF - (end - begin) :])
            else:
                nc.vector.tensor_copy(rows[:], sums[:, HALF - (end - begin) :])
            put(rows[:], c, begin, end)
        nc.sync.dma_start(out=out[:P, :], in_=pages[0][:])
        nc.scalar.dma_start(out=out[P:, :], in_=pages[1][:])
